import numpy as np
CORES = [65,73,81,89,97,105,113,121]
N = 8
F = 64
BOUND = 8688.9
def setup_inputs(rng):
    gr = rng.standard_normal((1, 128, N * F), dtype=np.float32) + rng.standard_normal((N, 128, N * F), dtype=np.float32)
    return {"gr": gr}
def setup_inputs_big(rng):
    d = setup_inputs(rng)
    for k in ("gr",): d[k] = (d[k].astype(np.float32) * 1024.0).astype(d[k].dtype)
    return d
def setup_inputs_small(rng):
    d = setup_inputs(rng)
    for k in ("gr",): d[k] = (d[k].astype(np.float32) * (1 / 1024.0)).astype(d[k].dtype)
    return d
def setup_inputs_apart(rng):
    d = setup_inputs(rng)
    f = (10.0 ** rng.permutation(np.linspace(-1.5, 1.5, N))).astype(np.float32).reshape(N, 1, 1)
    for k in ("gr",): d[k] = (d[k].astype(np.float32) * f).astype(d[k].dtype)
    return d
def setup_inputs_far(rng):
    d = setup_inputs(rng)
    for k in ("gr",): d[k] = (d[k].astype(np.float32) * 16384.0).astype(d[k].dtype)
    return d
def setup_inputs_over(rng):
    d = setup_inputs(rng)
    f = np.float32(10.0 ** rng.uniform(1.5, 3.5)) * np.where(rng.random((1, 128, N * F)) < 0.5, 0.1, 1.0).astype(np.float32)
    for k in ("gr",): d[k] = (d[k].astype(np.float32) * f).astype(d[k].dtype)
    return d
def reference(gr):
    s = gr.astype(np.float64).sum(axis=0)
    nrm = np.sqrt((s ** 2).sum())
    s = s * min(1.0, BOUND / nrm)
    return {"y": np.stack([s[:, F * r:F * r + F] for r in range(N)]).astype(np.float32)}

@@ -1,0 +1,217 @@
+from concourse.bass import DstId, RemoteDMATransfer
+from concourse.mybir import AluOpType, AxisListType, ActivationFunctionType
+
+P = 128
+F = 64
+W = 2 * F
+K1 = 63
+K2 = 64
+RHO = 4.0 ** (1.0 / K2)
+
+SCRATCH = {
+    "gin": ("sbuf", [P, 8 * F], "float32"),
+    "hp0": ("sbuf", [P, W], "float32"),
+    "ha": ("sbuf", [P, W], "float32"),
+    "hb": ("sbuf", [P, W], "float32"),
+    "hc": ("sbuf", [P, W], "float32"),
+    "hs1": ("sbuf", [P, W], "float32"),
+    "hs2": ("sbuf", [P, W], "float32"),
+    "la": ("sbuf", [P, W], "float32"),
+    "lbc": ("sbuf", [P, W], "float32"),
+    "ma": ("sbuf", [P, W], "float32"),
+    "mbc": ("sbuf", [P, W], "float32"),
+    "junk": ("sbuf", [P, W], "float32"),
+    "qown": ("sbuf", [P, 4], "float32"),
+    "qland": ("sbuf", [P, 4], "float32"),
+    "ones": ("sbuf", [P, P], "float32"),
+    "c4": ("sbuf", [P, K2], "float32"),
+    "cr": ("sbuf", [P, K2], "float32"),
+    "zz": ("sbuf", [P, K2], "float32"),
+    "thr1": ("sbuf", [P, K2], "float32"),
+    "thr2": ("sbuf", [P, K2], "float32"),
+    "m1": ("sbuf", [P, K2], "float32"),
+    "m2": ("sbuf", [P, K2], "float32"),
+    "clampv": ("sbuf", [P, 4], "float32"),
+    "sc4": ("sbuf", [P, 4], "float32"),
+    "sv": ("sbuf", [P, 8], "float32"),
+    "sy": ("sbuf", [P, F], "float32"),
+    "yo": ("sbuf", [P, F], "float32"),
+    "acc": ("psum", [P, 512], "float32"),
+    "ps": ("psum", [P, 512], "float32"),
+}
+SEMAPHORES = ["ldA", "ldB", "snd", "a0", "a1", "a23", "early", "late_o", "late_m", "qarr", "vs", "acts", "mms", "st"]
+
+
+def _bits(mask):
+    return [1 << b for b in range(mask.bit_length()) if (mask >> b) & 1]
+
+
+def _cnt(mask):
+    return len(_bits(mask))
+
+
+def _plan(T, topo):
+    cores = list(T.cores)
+    info = {}
+    for r, c in enumerate(cores):
+        mate = [d for d in cores if topo.mates(topo.chip(c), topo.chip(d))][0]
+        helper = [h for h in range(min(cores) - P, max(cores) + P)
+                  if h >= 0 and h not in cores and topo.chip(h) == topo.chip(c) and topo.die(h) == topo.die(c)
+                  and topo.may_write(h, mate)][0]
+        lo = min(r, cores.index(mate))
+        info[c] = {"rank": r, "mate": mate, "helper": helper, "off": F * lo, "half": F * (r - lo)}
+    for c in cores:
+        mem = [d for d in cores if d == c or topo.same_plane(topo.chip(c), topo.chip(d))]
+        mem.sort(key=lambda d: info[d]["off"])
+        info[c]["members"] = mem
+    return info
+
+
+def _dst(topo, c):
+    rid, pid, _ = topo.addr(c)
+    return DstId(rid=rid, pnc=pid)
+
+
+def _chain(queue, sem):
+    n = [0]
+
+    def run(make):
+        if n[0]:
+            queue.wait_ge(sem, n[0])
+        make().then_inc(sem, 1)
+        n[0] += 1
+        return n[0]
+    return run
+
+
+def _helper_program(g, core, T, topo, own, mate):
+    v = g.vector
+    S = T.sem
+    vop = _chain(v, S.vs)
+    low = topo.mask(core, mate)
+    high = topo.mask(core, own) & ~low
+    add = AluOpType.add
+
+    v.wait_ge(S.a0, _cnt(high))
+    v.wait_ge(S.a1, _cnt(low))
+    n = vop(lambda: v.tensor_tensor(T.hs1[:], T.hp0[:], T.ha[:], add))
+    g.wait_ge(S.a1, _cnt(low))
+    g.wait_ge(S.vs, n)
+    g.remote_dma_fused([
+        RemoteDMATransfer(dst_ids=[_dst(topo, mate)], dma_engine_mask=low, remote_sem=S.early, src=T.hs1[:], dst=T.ma[:]),
+        RemoteDMATransfer(dst_ids=[_dst(topo, own)], dma_engine_mask=high, remote_sem=S.early, src=T.ha[:], dst=T.la[:]),
+    ], local_sem=S.snd)
+
+    v.wait_ge(S.a23, _cnt(low))
+    n = vop(lambda: v.tensor_tensor(T.hs2[:], T.hb[:], T.hc[:], add))
+    g.wait_ge(S.vs, n)
+    g.remote_dma_fused([
+        RemoteDMATransfer(dst_ids=[_dst(topo, mate)], dma_engine_mask=low, remote_sem=S.late_m, src=T.hs2[:], dst=T.mbc[:]),
+        RemoteDMATransfer(dst_ids=[_dst(topo, own)], dma_engine_mask=high, remote_sem=S.late_o, src=T.hs2[:], dst=T.lbc[:]),
+    ], local_sem=S.snd)
+    g.wait_ge(S.snd, 2 * (_cnt(low) + _cnt(high)))
+
+
+def _rank_program(g, core, T, topo, info):
+    me = info[core]
+    mem = me["members"]
+    i = mem.index(core)
+    peer = [mem[i ^ j] for j in range(4)]
+    off = [info[c]["off"] for c in peer]
+    helper = [info[c]["helper"] for c in peer]
+    v, sc, te, sy = g.vector, g.scalar, g.tensor, g.sync
+    S = T.sem
+    A = AluOpType
+    vop = _chain(v, S.vs)
+    low = topo.mask(core, helper[1])
+    high = topo.mask(core, helper[0]) & ~low
+    lb = _bits(low)
+    low_a, low_b = sum(lb[:len(lb) // 2]), sum(lb[len(lb) // 2:])
+    bound = float(T.tables["BOUND"])
+
+    oa, ob = min(off[0], off[1]), min(off[2], off[3])
+    sy.dma_start(T.gin[:, oa:oa + 2 * W], T.gr[:, oa:oa + 2 * W]).then_inc(S.ldA, 16)
+    sy.dma_start(T.gin[:, ob:ob + 2 * W], T.gr[:, ob:ob + 2 * W]).then_inc(S.ldB, 16)
+
+    g.wait_ge(S.ldA, 16)
+    g.remote_dma_fused([
+        RemoteDMATransfer(dst_ids=[_dst(topo, helper[1])], dma_engine_mask=low, remote_sem=S.a1,
+                          src=T.gin[:, off[1]:off[1] + W], dst=T.ha[:]),
+        RemoteDMATransfer(dst_ids=[_dst(topo, helper[0])], dma_engine_mask=high, remote_sem=S.a0,
+                          src=T.gin[:, off[0]:off[0] + W], dst=T.hp0[:]),
+    ], local_sem=S.snd)
+    g.wait_ge(S.ldB, 16)
+    g.remote_dma_fused([
+        RemoteDMATransfer(dst_ids=[_dst(topo, helper[2])], dma_engine_mask=low_a, remote_sem=S.a23,
+                          src=T.gin[:, off[2]:off[2] + W], dst=T.hb[:]),
+        RemoteDMATransfer(dst_ids=[_dst(topo, helper[3])], dma_engine_mask=low_b, remote_sem=S.a23,
+                          src=T.gin[:, off[3]:off[3] + W], dst=T.hc[:]),
+    ], local_sem=S.snd)
+
+    vop(lambda: v.memset(T.ones[:], 1.0))
+    vop(lambda: v.memset(T.c4[:], 4.0))
+    vop(lambda: v.memset(T.cr[:], RHO))
+    vop(lambda: v.memset(T.zz[:], 0.0))
+    vop(lambda: v.memset(T.clampv[:], 0.0))
+    vop(lambda: v.memset(T.clampv[:, 3:4], 1.0))
+    vop(lambda: v.tensor_tensor_scan(T.thr1[:, 0:K1], T.c4[:, 0:K1], T.zz[:, 0:K1], 1.0, A.mult, A.add))
+    n_const = vop(lambda: v.tensor_tensor_scan(T.thr2[:], T.cr[:], T.zz[:], RHO ** -0.5, A.mult, A.add))
+
+    acc = T.acc[:, 0:W]
+    v.wait_ge(S.ldA, 16)
+    v.wait_ge(S.early, _cnt(low) + _cnt(high))
+    vop(lambda: v.tensor_tensor(acc, T.gin[:, off[0]:off[0] + W], T.la[:], A.add))
+    vop(lambda: v.tensor_tensor(acc, acc, T.ma[:], A.add))
+    v.wait_ge(S.late_o, _cnt(high))
+    vop(lambda: v.tensor_tensor(acc, acc, T.lbc[:], A.add))
+    v.wait_ge(S.late_m, _cnt(low))
+    n_sum = vop(lambda: v.tensor_tensor(acc, acc, T.mbc[:], A.add))
+
+    sc.wait_ge(S.vs, n_sum)
+    sc.activation(T.junk[:], acc, ActivationFunctionType.Square, scale=1.0 / bound,
+                  accum_out=T.qown[:, 0:1]).then_inc(S.acts, 1)
+
+    g.wait_ge(S.acts, 1)
+    g.remote_dma_fused([
+        RemoteDMATransfer(dst_ids=[_dst(topo, peer[j]) for j in (1, 2, 3)], dma_engine_mask=low, remote_sem=S.qarr,
+                          srcs=[T.qown[:, 0:1]], dsts=[T.qland[:, j - 1:j] for j in (1, 2, 3)]),
+    ], local_sem=S.snd)
+
+    te.wait_ge(S.vs, n_const)
+    te.wait_ge(S.acts, 1)
+    te.matmul(T.ps[:, 0:1], T.ones[:], T.qown[:, 0:1], True, True).then_inc(S.mms, 1)
+    te.wait_ge(S.qarr, 3 * _cnt(low))
+    te.matmul(T.ps[:, 1:4], T.ones[:], T.qland[:, 0:3], True, True).then_inc(S.mms, 1)
+
+    t, y0, t1, y1, a, p, p2 = (T.sc4[:, 3:4],) + tuple(T.sv[:, k:k + 1] for k in range(6))
+    v.wait_ge(S.mms, 2)
+    vop(lambda: v.tensor_tensor_scan(T.sc4[:], T.ps[:, 0:4], T.clampv[:], 0.0, A.add, A.max))
+    vop(lambda: v.tensor_scalar(T.m1[:, 0:K1], T.thr1[:, 0:K1], t, 0.5, A.is_gt, A.max))
+    n_y0 = vop(lambda: v.tensor_reduce(y0, T.m1[:, 0:K1], AxisListType.X, A.mult))
+    vop(lambda: v.tensor_scalar(t1, y0, y0, t, A.mult, A.mult))
+    vop(lambda: v.tensor_scalar(T.m2[:], T.thr2[:], t1, RHO ** -0.5, A.is_gt, A.max))
+    vop(lambda: v.tensor_reduce(y1, T.m2[:], AxisListType.X, A.mult))
+    vop(lambda: v.tensor_scalar(a, y1, y1, t1, A.mult, A.mult))
+    vop(lambda: v.tensor_scalar(p, a, 0.375, -1.25, A.mult, A.add))
+    vop(lambda: v.tensor_scalar(p2, p, a, 1.875, A.mult, A.add))
+    h = me["half"]
+    sc.wait_ge(S.vs, n_y0)
+    sc.activation(T.sy[:], T.acc[:, h:h + F], ActivationFunctionType.Copy, scale=y0).then_inc(S.acts, 1)
+    v.wait_ge(S.acts, 2)
+    n_out = vop(lambda: v.tensor_scalar(T.yo[:], T.sy[:], y1, p2, A.mult, A.mult))
+
+    sy.wait_ge(S.vs, n_out)
+    sy.dma_start(T.y[:], T.yo[:]).then_inc(S.st, 16)
+    sy.wait_ge(S.st, 16)
+    g.wait_ge(S.snd, _cnt(low) + _cnt(high) + _cnt(low_a) + _cnt(low_b) + _cnt(low))
+
+
+def rank_program(g, core, T, topo):
+    info = _plan(T, topo)
+    if core in info:
+        _rank_program(g, core, T, topo, info)
+        return
+    for c in info:
+        if info[c]["helper"] == core:
+            _helper_program(g, core, T, topo, c, info[c]["mate"])
+            return

@@ -5,41 +5,43 @@ P = 128
 F = 64
 W = 2 * F
 K1 = 63
-K2 = 64
-RHO = 4.0 ** (1.0 / K2)
+COEF = [0.0003236419870518148, -0.0005557614495046437, -0.0002574043464846909, 0.0004350104427430779,
+        0.0010859891772270203, -0.0018878575647249818, 0.0019057323224842548, -0.0033998521976172924,
+        0.006695993710309267, -0.012170334346592426, 0.022408906370401382, -0.04268435388803482,
+        0.08538159728050232, -0.18973682820796967, 0.6324555277824402]
+NC = len(COEF)
 
 SCRATCH = {
     "gin": ("sbuf", [P, 8 * F], "float32"),
     "hp0": ("sbuf", [P, W], "float32"),
-    "ha": ("sbuf", [P, W], "float32"),
-    "hb": ("sbuf", [P, W], "float32"),
-    "hc": ("sbuf", [P, W], "float32"),
-    "hs1": ("sbuf", [P, W], "float32"),
-    "hs2": ("sbuf", [P, W], "float32"),
-    "la": ("sbuf", [P, W], "float32"),
-    "lbc": ("sbuf", [P, W], "float32"),
-    "ma": ("sbuf", [P, W], "float32"),
-    "mbc": ("sbuf", [P, W], "float32"),
+    "hx1": ("sbuf", [P, W], "float32"),
+    "hx2": ("sbuf", [P, W], "float32"),
+    "hx3": ("sbuf", [P, W], "float32"),
+    "hE": ("sbuf", [P, W], "float32"),
+    "hacc": ("psum", [P, 512], "float32"),
+    "lE": ("sbuf", [P, W], "float32"),
+    "mO": ("sbuf", [P, W], "float32"),
     "junk": ("sbuf", [P, W], "float32"),
     "qown": ("sbuf", [P, 4], "float32"),
-    "qland": ("sbuf", [P, 4], "float32"),
+    "qland": ("sbuf", [P, 8], "float32"),
     "ones": ("sbuf", [P, P], "float32"),
-    "c4": ("sbuf", [P, K2], "float32"),
-    "cr": ("sbuf", [P, K2], "float32"),
-    "zz": ("sbuf", [P, K2], "float32"),
-    "thr1": ("sbuf", [P, K2], "float32"),
-    "thr2": ("sbuf", [P, K2], "float32"),
-    "m1": ("sbuf", [P, K2], "float32"),
-    "m2": ("sbuf", [P, K2], "float32"),
-    "clampv": ("sbuf", [P, 4], "float32"),
-    "sc4": ("sbuf", [P, 4], "float32"),
-    "sv": ("sbuf", [P, 8], "float32"),
-    "sy": ("sbuf", [P, F], "float32"),
+    "c4": ("sbuf", [P, F], "float32"),
+    "zz": ("sbuf", [P, F], "float32"),
+    "thr1": ("sbuf", [P, F], "float32"),
+    "m1": ("sbuf", [P, F], "float32"),
+    "clampv": ("sbuf", [P, 8], "float32"),
+    "sc8": ("sbuf", [P, 8], "float32"),
+    "sv": ("sbuf", [P, 4], "float32"),
+    "arow": ("sbuf", [P, 16], "float32"),
+    "urow": ("sbuf", [P, 16], "float32"),
+    "coef": ("sbuf", [P, 16], "float32"),
+    "hrow": ("sbuf", [P, 16], "float32"),
     "yo": ("sbuf", [P, F], "float32"),
-    "acc": ("psum", [P, 512], "float32"),
+    "accA": ("psum", [P, 512], "float32"),
+    "accB": ("psum", [P, 512], "float32"),
     "ps": ("psum", [P, 512], "float32"),
 }
-SEMAPHORES = ["ldA", "ldB", "snd", "a0", "a1", "a23", "early", "late_o", "late_m", "qarr", "vs", "acts", "mms", "st"]
+SEMAPHORES = ["ldA", "ldB", "snd", "tab", "a0", "a1", "a23", "late_o", "late_m", "qarr", "vs", "acts", "mms", "st"]
 
 
 def _bits(mask):
@@ -59,7 +61,7 @@ def _plan(T, topo):
                   if h >= 0 and h not in cores and topo.chip(h) == topo.chip(c) and topo.die(h) == topo.die(c)
                   and topo.may_write(h, mate)][0]
         lo = min(r, cores.index(mate))
-        info[c] = {"rank": r, "mate": mate, "helper": helper, "off": F * lo, "half": F * (r - lo)}
+        info[c] = {"rank": r, "mate": mate, "helper": helper, "off": F * lo, "half": r - lo}
     for c in cores:
         mem = [d for d in cores if d == c or topo.same_plane(topo.chip(c), topo.chip(d))]
         mem.sort(key=lambda d: info[d]["off"])
@@ -91,23 +93,25 @@ def _helper_program(g, core, T, topo, own, mate):
     low = topo.mask(core, mate)
     high = topo.mask(core, own) & ~low
     add = AluOpType.add
+    acc = T.hacc[:, 0:W]
 
-    v.wait_ge(S.a0, _cnt(high))
-    v.wait_ge(S.a1, _cnt(low))
-    n = vop(lambda: v.tensor_tensor(T.hs1[:], T.hp0[:], T.ha[:], add))
-    g.wait_ge(S.a1, _cnt(low))
+    n = vop(lambda: v.memset(T.ones[:], 1.0))
     g.wait_ge(S.vs, n)
     g.remote_dma_fused([
-        RemoteDMATransfer(dst_ids=[_dst(topo, mate)], dma_engine_mask=low, remote_sem=S.early, src=T.hs1[:], dst=T.ma[:]),
-        RemoteDMATransfer(dst_ids=[_dst(topo, own)], dma_engine_mask=high, remote_sem=S.early, src=T.ha[:], dst=T.la[:]),
+        RemoteDMATransfer(dst_ids=[_dst(topo, own)], dma_engine_mask=low | high, remote_sem=S.tab,
+                          src=T.ones[:], dst=T.ones[:]),
     ], local_sem=S.snd)
 
     v.wait_ge(S.a23, _cnt(low))
-    n = vop(lambda: v.tensor_tensor(T.hs2[:], T.hb[:], T.hc[:], add))
+    vop(lambda: v.tensor_tensor(acc, T.hx2[:], T.hx3[:], add))
+    v.wait_ge(S.a0, _cnt(high))
+    vop(lambda: v.tensor_tensor(acc, acc, T.hp0[:], add))
+    v.wait_ge(S.a1, _cnt(low))
+    n = vop(lambda: v.tensor_tensor(T.hE[:], acc, T.hx1[:], add))
     g.wait_ge(S.vs, n)
     g.remote_dma_fused([
-        RemoteDMATransfer(dst_ids=[_dst(topo, mate)], dma_engine_mask=low, remote_sem=S.late_m, src=T.hs2[:], dst=T.mbc[:]),
-        RemoteDMATransfer(dst_ids=[_dst(topo, own)], dma_engine_mask=high, remote_sem=S.late_o, src=T.hs2[:], dst=T.lbc[:]),
+        RemoteDMATransfer(dst_ids=[_dst(topo, mate)], dma_engine_mask=low, remote_sem=S.late_m, src=T.hE[:], dst=T.mO[:]),
+        RemoteDMATransfer(dst_ids=[_dst(topo, own)], dma_engine_mask=high, remote_sem=S.late_o, src=T.hE[:], dst=T.lE[:]),
     ], local_sem=S.snd)
     g.wait_ge(S.snd, 2 * (_cnt(low) + _cnt(high)))
 
@@ -122,6 +126,7 @@ def _rank_program(g, core, T, topo, info):
     v, sc, te, sy = g.vector, g.scalar, g.tensor, g.sync
     S = T.sem
     A = AluOpType
+    Act = ActivationFunctionType
     vop = _chain(v, S.vs)
     low = topo.mask(core, helper[1])
     high = topo.mask(core, helper[0]) & ~low
@@ -129,81 +134,72 @@ def _rank_program(g, core, T, topo, info):
     low_a, low_b = sum(lb[:len(lb) // 2]), sum(lb[len(lb) // 2:])
     bound = float(T.tables["BOUND"])
 
-    oa, ob = min(off[0], off[1]), min(off[2], off[3])
+    oa, ob = min(off[2], off[3]), min(off[0], off[1])
     sy.dma_start(T.gin[:, oa:oa + 2 * W], T.gr[:, oa:oa + 2 * W]).then_inc(S.ldA, 16)
-    sy.dma_start(T.gin[:, ob:ob + 2 * W], T.gr[:, ob:ob + 2 * W]).then_inc(S.ldB, 16)
+    sc.dma_start(T.gin[:, ob:ob + 2 * W], T.gr[:, ob:ob + 2 * W]).then_inc(S.ldB, 16)
 
     g.wait_ge(S.ldA, 16)
     g.remote_dma_fused([
-        RemoteDMATransfer(dst_ids=[_dst(topo, helper[1])], dma_engine_mask=low, remote_sem=S.a1,
-                          src=T.gin[:, off[1]:off[1] + W], dst=T.ha[:]),
-        RemoteDMATransfer(dst_ids=[_dst(topo, helper[0])], dma_engine_mask=high, remote_sem=S.a0,
-                          src=T.gin[:, off[0]:off[0] + W], dst=T.hp0[:]),
+        RemoteDMATransfer(dst_ids=[_dst(topo, helper[2])], dma_engine_mask=low_a, remote_sem=S.a23,
+                          src=T.gin[:, off[2]:off[2] + W], dst=T.hx2[:]),
+        RemoteDMATransfer(dst_ids=[_dst(topo, helper[3])], dma_engine_mask=low_b, remote_sem=S.a23,
+                          src=T.gin[:, off[3]:off[3] + W], dst=T.hx3[:]),
     ], local_sem=S.snd)
     g.wait_ge(S.ldB, 16)
     g.remote_dma_fused([
-        RemoteDMATransfer(dst_ids=[_dst(topo, helper[2])], dma_engine_mask=low_a, remote_sem=S.a23,
-                          src=T.gin[:, off[2]:off[2] + W], dst=T.hb[:]),
-        RemoteDMATransfer(dst_ids=[_dst(topo, helper[3])], dma_engine_mask=low_b, remote_sem=S.a23,
-                          src=T.gin[:, off[3]:off[3] + W], dst=T.hc[:]),
+        RemoteDMATransfer(dst_ids=[_dst(topo, helper[1])], dma_engine_mask=low, remote_sem=S.a1,
+                          src=T.gin[:, off[1]:off[1] + W], dst=T.hx1[:]),
+        RemoteDMATransfer(dst_ids=[_dst(topo, helper[0])], dma_engine_mask=high, remote_sem=S.a0,
+                          src=T.gin[:, off[0]:off[0] + W], dst=T.hp0[:]),
     ], local_sem=S.snd)
 
-    vop(lambda: v.memset(T.ones[:], 1.0))
     vop(lambda: v.memset(T.c4[:], 4.0))
-    vop(lambda: v.memset(T.cr[:], RHO))
     vop(lambda: v.memset(T.zz[:], 0.0))
     vop(lambda: v.memset(T.clampv[:], 0.0))
-    vop(lambda: v.memset(T.clampv[:, 3:4], 1.0))
+    vop(lambda: v.memset(T.clampv[:, 7:8], 1.0))
+    vop(lambda: v.memset(T.arow[:], 1.0 / 1.5))
+    for k in range(NC):
+        vop(lambda: v.memset(T.coef[:, k:k + 1], COEF[k]))
     vop(lambda: v.tensor_tensor_scan(T.thr1[:, 0:K1], T.c4[:, 0:K1], T.zz[:, 0:K1], 1.0, A.mult, A.add))
-    n_const = vop(lambda: v.tensor_tensor_scan(T.thr2[:], T.cr[:], T.zz[:], RHO ** -0.5, A.mult, A.add))
 
-    acc = T.acc[:, 0:W]
-    v.wait_ge(S.ldA, 16)
-    v.wait_ge(S.early, _cnt(low) + _cnt(high))
-    vop(lambda: v.tensor_tensor(acc, T.gin[:, off[0]:off[0] + W], T.la[:], A.add))
-    vop(lambda: v.tensor_tensor(acc, acc, T.ma[:], A.add))
-    v.wait_ge(S.late_o, _cnt(high))
-    vop(lambda: v.tensor_tensor(acc, acc, T.lbc[:], A.add))
+    accs = (T.accA[:, 0:F], T.accB[:, 0:F])
+    sc.wait_ge(S.late_o, _cnt(high))
+    sc.activation(accs[0], T.lE[:, 0:F], Act.Copy).then_inc(S.acts, 1)
+    sc.activation(accs[1], T.lE[:, F:W], Act.Copy).then_inc(S.acts, 1)
     v.wait_ge(S.late_m, _cnt(low))
-    n_sum = vop(lambda: v.tensor_tensor(acc, acc, T.mbc[:], A.add))
+    for k in range(2):
+        v.wait_ge(S.acts, k + 1)
+        n = vop(lambda: v.tensor_tensor(accs[k], accs[k], T.mO[:, k * F:(k + 1) * F], A.add))
+        sc.wait_ge(S.vs, n)
+        sc.activation(T.junk[:, k * F:(k + 1) * F], accs[k], Act.Square, scale=1.0 / bound,
+                      accum_out=T.qown[:, k:k + 1]).then_inc(S.acts, 1)
 
-    sc.wait_ge(S.vs, n_sum)
-    sc.activation(T.junk[:], acc, ActivationFunctionType.Square, scale=1.0 / bound,
-                  accum_out=T.qown[:, 0:1]).then_inc(S.acts, 1)
-
-    g.wait_ge(S.acts, 1)
+    g.wait_ge(S.acts, 4)
     g.remote_dma_fused([
         RemoteDMATransfer(dst_ids=[_dst(topo, peer[j]) for j in (1, 2, 3)], dma_engine_mask=low, remote_sem=S.qarr,
-                          srcs=[T.qown[:, 0:1]], dsts=[T.qland[:, j - 1:j] for j in (1, 2, 3)]),
+                          srcs=[T.qown[:, 0:2]], dsts=[T.qland[:, 2 * j - 2:2 * j] for j in (1, 2, 3)]),
     ], local_sem=S.snd)
 
-    te.wait_ge(S.vs, n_const)
-    te.wait_ge(S.acts, 1)
-    te.matmul(T.ps[:, 0:1], T.ones[:], T.qown[:, 0:1], True, True).then_inc(S.mms, 1)
+    te.wait_ge(S.tab, _cnt(low) + _cnt(high))
+    te.wait_ge(S.acts, 4)
+    te.matmul(T.ps[:, 0:2], T.ones[:], T.qown[:, 0:2], True, True).then_inc(S.mms, 1)
     te.wait_ge(S.qarr, 3 * _cnt(low))
-    te.matmul(T.ps[:, 1:4], T.ones[:], T.qland[:, 0:3], True, True).then_inc(S.mms, 1)
+    te.matmul(T.ps[:, 2:8], T.ones[:], T.qland[:, 0:6], True, True).then_inc(S.mms, 1)
 
-    t, y0, t1, y1, a, p, p2 = (T.sc4[:, 3:4],) + tuple(T.sv[:, k:k + 1] for k in range(6))
+    t, y0, t1, hv = T.sc8[:, 7:8], T.sv[:, 0:1], T.sv[:, 1:2], T.hrow[:, NC - 1:NC]
     v.wait_ge(S.mms, 2)
-    vop(lambda: v.tensor_tensor_scan(T.sc4[:], T.ps[:, 0:4], T.clampv[:], 0.0, A.add, A.max))
+    vop(lambda: v.tensor_tensor_scan(T.sc8[:], T.ps[:, 0:8], T.clampv[:], 0.0, A.add, A.max))
     vop(lambda: v.tensor_scalar(T.m1[:, 0:K1], T.thr1[:, 0:K1], t, 0.5, A.is_gt, A.max))
-    n_y0 = vop(lambda: v.tensor_reduce(y0, T.m1[:, 0:K1], AxisListType.X, A.mult))
+    vop(lambda: v.tensor_reduce(y0, T.m1[:, 0:K1], AxisListType.X, A.mult))
     vop(lambda: v.tensor_scalar(t1, y0, y0, t, A.mult, A.mult))
-    vop(lambda: v.tensor_scalar(T.m2[:], T.thr2[:], t1, RHO ** -0.5, A.is_gt, A.max))
-    vop(lambda: v.tensor_reduce(y1, T.m2[:], AxisListType.X, A.mult))
-    vop(lambda: v.tensor_scalar(a, y1, y1, t1, A.mult, A.mult))
-    vop(lambda: v.tensor_scalar(p, a, 0.375, -1.25, A.mult, A.add))
-    vop(lambda: v.tensor_scalar(p2, p, a, 1.875, A.mult, A.add))
-    h = me["half"]
-    sc.wait_ge(S.vs, n_y0)
-    sc.activation(T.sy[:], T.acc[:, h:h + F], ActivationFunctionType.Copy, scale=y0).then_inc(S.acts, 1)
-    v.wait_ge(S.acts, 2)
-    n_out = vop(lambda: v.tensor_scalar(T.yo[:], T.sy[:], y1, p2, A.mult, A.mult))
+    vop(lambda: v.tensor_scalar(T.urow[:, 0:NC], T.arow[:, 0:NC], t1, -2.5 / 1.5, A.mult, A.add))
+    vop(lambda: v.tensor_tensor_scan(T.hrow[:, 0:NC], T.urow[:, 0:NC], T.coef[:, 0:NC], 0.0, A.mult, A.add))
+    n_out = vop(lambda: v.tensor_scalar(T.yo[:], accs[me["half"]], y0, hv, A.mult, A.mult))
 
     sy.wait_ge(S.vs, n_out)
     sy.dma_start(T.y[:], T.yo[:]).then_inc(S.st, 16)
     sy.wait_ge(S.st, 16)
-    g.wait_ge(S.snd, _cnt(low) + _cnt(high) + _cnt(low_a) + _cnt(low_b) + _cnt(low))
+    g.wait_ge(S.snd, _cnt(low_a) + _cnt(low_b) + _cnt(low) + _cnt(high) + _cnt(low))
 
 
 def rank_program(g, core, T, topo):

@@ -32,6 +32,7 @@ SCRATCH = {
     "clampv": ("sbuf", [P, 8], "float32"),
     "sc8": ("sbuf", [P, 8], "float32"),
     "sv": ("sbuf", [P, 4], "float32"),
+    "asrc": ("sbuf", [P, 16], "float32"),
     "arow": ("sbuf", [P, 16], "float32"),
     "urow": ("sbuf", [P, 16], "float32"),
     "coef": ("sbuf", [P, 16], "float32"),
@@ -41,7 +42,7 @@ SCRATCH = {
     "accB": ("psum", [P, 512], "float32"),
     "ps": ("psum", [P, 512], "float32"),
 }
-SEMAPHORES = ["ldA", "ldB", "snd", "tab", "a0", "a1", "a23", "late_o", "late_m", "qarr", "vs", "acts", "mms", "st"]
+SEMAPHORES = ["ldA", "ldB", "snd", "tab", "tabr", "a0", "a1", "a23", "late_o", "late_m", "qarr", "vs", "acts", "mms", "st"]
 
 
 def _bits(mask):
@@ -138,6 +139,13 @@ def _rank_program(g, core, T, topo, info):
     sy.dma_start(T.gin[:, oa:oa + 2 * W], T.gr[:, oa:oa + 2 * W]).then_inc(S.ldA, 16)
     sc.dma_start(T.gin[:, ob:ob + 2 * W], T.gr[:, ob:ob + 2 * W]).then_inc(S.ldB, 16)
 
+    n = vop(lambda: v.memset(T.asrc[:], 1.0 / 1.5))
+    g.wait_ge(S.vs, n)
+    g.remote_dma_fused([
+        RemoteDMATransfer(dst_ids=[_dst(topo, peer[1])], dma_engine_mask=low, remote_sem=S.tabr,
+                          src=T.asrc[:], dst=T.arow[:]),
+    ], local_sem=S.snd)
+
     g.wait_ge(S.ldA, 16)
     g.remote_dma_fused([
         RemoteDMATransfer(dst_ids=[_dst(topo, helper[2])], dma_engine_mask=low_a, remote_sem=S.a23,
@@ -157,7 +165,6 @@ def _rank_program(g, core, T, topo, info):
     vop(lambda: v.memset(T.zz[:], 0.0))
     vop(lambda: v.memset(T.clampv[:], 0.0))
     vop(lambda: v.memset(T.clampv[:, 7:8], 1.0))
-    vop(lambda: v.memset(T.arow[:], 1.0 / 1.5))
     for k in range(NC):
         vop(lambda: v.memset(T.coef[:, k:k + 1], COEF[k]))
     vop(lambda: v.tensor_tensor_scan(T.thr1[:, 0:K1], T.c4[:, 0:K1], T.zz[:, 0:K1], 1.0, A.mult, A.add))
@@ -166,6 +173,7 @@ def _rank_program(g, core, T, topo, info):
     sc.wait_ge(S.late_o, _cnt(high))
     sc.activation(accs[0], T.lE[:, 0:F], Act.Copy).then_inc(S.acts, 1)
     sc.activation(accs[1], T.lE[:, F:W], Act.Copy).then_inc(S.acts, 1)
+    v.wait_ge(S.tabr, _cnt(low))
     v.wait_ge(S.late_m, _cnt(low))
     for k in range(2):
         v.wait_ge(S.acts, k + 1)
@@ -199,7 +207,7 @@ def _rank_program(g, core, T, topo, info):
     sy.wait_ge(S.vs, n_out)
     sy.dma_start(T.y[:], T.yo[:]).then_inc(S.st, 16)
     sy.wait_ge(S.st, 16)
-    g.wait_ge(S.snd, _cnt(low_a) + _cnt(low_b) + _cnt(low) + _cnt(high) + _cnt(low))
+    g.wait_ge(S.snd, _cnt(low) + _cnt(low_a) + _cnt(low_b) + _cnt(low) + _cnt(high) + _cnt(low))
 
 
 def rank_program(g, core, T, topo):

@@ -1,15 +1,42 @@
+import numpy as np
 from concourse.bass import DstId, RemoteDMATransfer
-from concourse.mybir import AluOpType, AxisListType, ActivationFunctionType
+from concourse.mybir import AluOpType, ActivationFunctionType
 
 P = 128
 F = 64
 W = 2 * F
-K1 = 63
-COEF = [0.0003236419870518148, -0.0005557614495046437, -0.0002574043464846909, 0.0004350104427430779,
-        0.0010859891772270203, -0.0018878575647249818, 0.0019057323224842548, -0.0033998521976172924,
-        0.006695993710309267, -0.012170334346592426, 0.022408906370401382, -0.04268435388803482,
-        0.08538159728050232, -0.18973682820796967, 0.6324555277824402]
-NC = len(COEF)
+K = 31
+DEG = 28
+NC = DEG + 1
+TC = 2 * K
+L = TC + 1 + NC
+
+
+def _leja(x):
+    x = list(x)
+    o = [max(x, key=abs)]
+    x.remove(o[0])
+    while x:
+        b = max(x, key=lambda v: np.sum(np.log(np.abs(v - np.array(o)))))
+        o.append(b)
+        x.remove(b)
+    return np.array(o)
+
+
+def _newton():
+    k = np.arange(NC)
+    x = np.round(_leja(np.cos(np.pi * (k + 0.5) / NC)) * 4096) / 4096
+    c = np.array((8.5 + 7.5 * x) ** -0.5, dtype=np.longdouble)
+    xl = x.astype(np.longdouble)
+    for j in range(1, NC):
+        c[j:] = (c[j:] - c[j - 1:-1]) / (xl[j:] - xl[:-j])
+    xs = [x[NC - 2]] + [x[j] for j in range(NC - 2, -1, -1)]
+    shift = [-8.5 / 7.5 - xs[0]] + [xs[i - 1] - xs[i] for i in range(1, NC)]
+    coef = [c[j] for j in range(NC - 1, -1, -1)]
+    return [float(v) for v in shift], [float(v) for v in coef]
+
+
+SHIFT, COEF = _newton()
 
 SCRATCH = {
     "gin": ("sbuf", [P, 8 * F], "float32"),
@@ -25,24 +52,22 @@ SCRATCH = {
     "qown": ("sbuf", [P, 4], "float32"),
     "qland": ("sbuf", [P, 8], "float32"),
     "ones": ("sbuf", [P, P], "float32"),
-    "c4": ("sbuf", [P, F], "float32"),
-    "zz": ("sbuf", [P, F], "float32"),
-    "thr1": ("sbuf", [P, F], "float32"),
-    "m1": ("sbuf", [P, F], "float32"),
+    "c16": ("sbuf", [P, 32], "float32"),
+    "thr2": ("sbuf", [P, 64], "float32"),
     "clampv": ("sbuf", [P, 8], "float32"),
-    "sc8": ("sbuf", [P, 8], "float32"),
-    "sv": ("sbuf", [P, 4], "float32"),
-    "asrc": ("sbuf", [P, 16], "float32"),
-    "arow": ("sbuf", [P, 16], "float32"),
-    "urow": ("sbuf", [P, 16], "float32"),
-    "coef": ("sbuf", [P, 16], "float32"),
-    "hrow": ("sbuf", [P, 16], "float32"),
+    "asrc": ("sbuf", [P, 32], "float32"),
+    "mrow": ("sbuf", [P, 96], "float32"),
+    "drow": ("sbuf", [P, 96], "float32"),
+    "orow": ("sbuf", [P, 96], "float32"),
+    "coef": ("sbuf", [P, 32], "float32"),
+    "hrow": ("sbuf", [P, 32], "float32"),
     "yo": ("sbuf", [P, F], "float32"),
     "accA": ("psum", [P, 512], "float32"),
     "accB": ("psum", [P, 512], "float32"),
     "ps": ("psum", [P, 512], "float32"),
 }
-SEMAPHORES = ["ldA", "ldB", "snd", "tab", "tabr", "a0", "a1", "a23", "late_o", "late_m", "qarr", "vs", "acts", "mms", "st"]
+SEMAPHORES = ["ldA", "ldB", "snd", "tab", "tabr", "a0", "a1", "a23", "late_o", "late_m", "qarr", "vs", "vb", "w0", "cv",
+              "cst", "acts", "mms", "st"]
 
 
 def _bits(mask):
@@ -139,11 +164,11 @@ def _rank_program(g, core, T, topo, info):
     sy.dma_start(T.gin[:, oa:oa + 2 * W], T.gr[:, oa:oa + 2 * W]).then_inc(S.ldA, 16)
     sc.dma_start(T.gin[:, ob:ob + 2 * W], T.gr[:, ob:ob + 2 * W]).then_inc(S.ldB, 16)
 
-    n = vop(lambda: v.memset(T.asrc[:], 1.0 / 1.5))
-    g.wait_ge(S.vs, n)
+    v.memset(T.asrc[:], 1.0).then_inc(S.w0, 1)
+    g.wait_ge(S.w0, 1)
     g.remote_dma_fused([
         RemoteDMATransfer(dst_ids=[_dst(topo, peer[1])], dma_engine_mask=low, remote_sem=S.tabr,
-                          src=T.asrc[:], dst=T.arow[:]),
+                          src=T.asrc[:], dst=T.mrow[:, TC + 2:TC + 2 + 32]),
     ], local_sem=S.snd)
 
     g.wait_ge(S.ldA, 16)
@@ -161,26 +186,35 @@ def _rank_program(g, core, T, topo, info):
                           src=T.gin[:, off[0]:off[0] + W], dst=T.hp0[:]),
     ], local_sem=S.snd)
 
-    vop(lambda: v.memset(T.c4[:], 4.0))
-    vop(lambda: v.memset(T.zz[:], 0.0))
-    vop(lambda: v.memset(T.clampv[:], 0.0))
-    vop(lambda: v.memset(T.clampv[:, 7:8], 1.0))
+    fills = [(T.c16[:], 16.0), (T.drow[:, 0:TC + 1], 0.0), (T.clampv[:, 0:7], 0.0), (T.clampv[:, 7:8], 1.0),
+             (T.mrow[:, TC + 1:TC + 2], 1.0 / 7.5)]
+    fills += [(T.coef[:, k:k + 1], COEF[k]) for k in range(NC)]
+    for ap, val in fills:
+        v.memset(ap, val).then_inc(S.cv, 1)
+    v.wait_ge(S.cv, len(fills))
+    for k in range(2):
+        v.tensor_tensor_scan(T.thr2[:, k * K:(k + 1) * K], T.c16[:, 0:K], T.drow[:, 0:K], 1.0, A.mult, A.add).then_inc(S.cv, 1)
+    sc.wait_ge(S.w0, 1)
     for k in range(NC):
-        vop(lambda: v.memset(T.coef[:, k:k + 1], COEF[k]))
-    vop(lambda: v.tensor_tensor_scan(T.thr1[:, 0:K1], T.c4[:, 0:K1], T.zz[:, 0:K1], 1.0, A.mult, A.add))
+        sc.activation(T.drow[:, TC + 1 + k:TC + 2 + k], T.asrc[:, 0:1], Act.Identity, bias=SHIFT[k],
+                      scale=0.0).then_inc(S.cst, 1)
 
     accs = (T.accA[:, 0:F], T.accB[:, 0:F])
     sc.wait_ge(S.late_o, _cnt(high))
     sc.activation(accs[0], T.lE[:, 0:F], Act.Copy).then_inc(S.acts, 1)
     sc.activation(accs[1], T.lE[:, F:W], Act.Copy).then_inc(S.acts, 1)
+    v.wait_ge(S.cv, len(fills) + 2)
+    v.wait_ge(S.cst, NC)
     v.wait_ge(S.tabr, _cnt(low))
     v.wait_ge(S.late_m, _cnt(low))
-    for k in range(2):
-        v.wait_ge(S.acts, k + 1)
-        n = vop(lambda: v.tensor_tensor(accs[k], accs[k], T.mO[:, k * F:(k + 1) * F], A.add))
-        sc.wait_ge(S.vs, n)
-        sc.activation(T.junk[:, k * F:(k + 1) * F], accs[k], Act.Square, scale=1.0 / bound,
-                      accum_out=T.qown[:, k:k + 1]).then_inc(S.acts, 1)
+    v.wait_ge(S.acts, 1)
+    n = vop(lambda: v.tensor_tensor(accs[0], accs[0], T.mO[:, 0:F], A.add))
+    v.wait_ge(S.acts, 2)
+    v.tensor_tensor(accs[1], accs[1], T.mO[:, F:W], A.add).then_inc(S.vb, 1)
+    sc.wait_ge(S.vs, n)
+    sc.activation(T.junk[:, 0:F], accs[0], Act.Square, scale=1.0 / bound, accum_out=T.qown[:, 0:1]).then_inc(S.acts, 1)
+    sc.wait_ge(S.vb, 1)
+    sc.activation(T.junk[:, F:W], accs[1], Act.Square, scale=1.0 / bound, accum_out=T.qown[:, 1:2]).then_inc(S.acts, 1)
 
     g.wait_ge(S.acts, 4)
     g.remote_dma_fused([
@@ -194,14 +228,12 @@ def _rank_program(g, core, T, topo, info):
     te.wait_ge(S.qarr, 3 * _cnt(low))
     te.matmul(T.ps[:, 2:8], T.ones[:], T.qland[:, 0:6], True, True).then_inc(S.mms, 1)
 
-    t, y0, t1, hv = T.sc8[:, 7:8], T.sv[:, 0:1], T.sv[:, 1:2], T.hrow[:, NC - 1:NC]
+    t, y0, hv = T.mrow[:, TC:TC + 1], T.orow[:, K - 1:K], T.hrow[:, NC - 1:NC]
     v.wait_ge(S.mms, 2)
-    vop(lambda: v.tensor_tensor_scan(T.sc8[:], T.ps[:, 0:8], T.clampv[:], 0.0, A.add, A.max))
-    vop(lambda: v.tensor_scalar(T.m1[:, 0:K1], T.thr1[:, 0:K1], t, 0.5, A.is_gt, A.max))
-    vop(lambda: v.tensor_reduce(y0, T.m1[:, 0:K1], AxisListType.X, A.mult))
-    vop(lambda: v.tensor_scalar(t1, y0, y0, t, A.mult, A.mult))
-    vop(lambda: v.tensor_scalar(T.urow[:, 0:NC], T.arow[:, 0:NC], t1, -2.5 / 1.5, A.mult, A.add))
-    vop(lambda: v.tensor_tensor_scan(T.hrow[:, 0:NC], T.urow[:, 0:NC], T.coef[:, 0:NC], 0.0, A.mult, A.add))
+    vop(lambda: v.tensor_tensor_scan(T.mrow[:, TC - 7:TC + 1], T.ps[:, 0:8], T.clampv[:], 0.0, A.add, A.max))
+    vop(lambda: v.tensor_scalar(T.mrow[:, 0:TC], T.thr2[:, 0:TC], t, 0.25, A.is_gt, A.max))
+    vop(lambda: v.tensor_tensor_scan(T.orow[:, 0:L], T.mrow[:, 0:L], T.drow[:, 0:L], 1.0, A.mult, A.add))
+    vop(lambda: v.tensor_tensor_scan(T.hrow[:, 0:NC], T.orow[:, TC + 1:L], T.coef[:, 0:NC], 0.0, A.mult, A.add))
     n_out = vop(lambda: v.tensor_scalar(T.yo[:], accs[me["half"]], y0, hv, A.mult, A.mult))
 
     sy.wait_ge(S.vs, n_out)

import numpy as np
from concourse.bass import DstId, RemoteDMATransfer
from concourse.mybir import AluOpType, ActivationFunctionType

P = 128
F = 64
W = 2 * F
K = 31
DEG = 28
NC = DEG + 1
TC = 2 * K
L = TC + 1 + NC


def _leja(x):
    x = list(x)
    o = [max(x, key=abs)]
    x.remove(o[0])
    while x:
        b = max(x, key=lambda v: np.sum(np.log(np.abs(v - np.array(o)))))
        o.append(b)
        x.remove(b)
    return np.array(o)


def _newton():
    k = np.arange(NC)
    x = np.round(_leja(np.cos(np.pi * (k + 0.5) / NC)) * 4096) / 4096
    c = np.array((8.5 + 7.5 * x) ** -0.5, dtype=np.longdouble)
    xl = x.astype(np.longdouble)
    for j in range(1, NC):
        c[j:] = (c[j:] - c[j - 1:-1]) / (xl[j:] - xl[:-j])
    xs = [x[NC - 2]] + [x[j] for j in range(NC - 2, -1, -1)]
    shift = [-8.5 / 7.5 - xs[0]] + [xs[i - 1] - xs[i] for i in range(1, NC)]
    coef = [c[j] for j in range(NC - 1, -1, -1)]
    return [float(v) for v in shift], [float(v) for v in coef]


SHIFT, COEF = _newton()

SCRATCH = {
    "gin": ("sbuf", [P, 8 * F], "float32"),
    "hp0": ("sbuf", [P, W], "float32"),
    "hx1": ("sbuf", [P, W], "float32"),
    "hx2": ("sbuf", [P, W], "float32"),
    "hx3": ("sbuf", [P, W], "float32"),
    "hE": ("sbuf", [P, W], "float32"),
    "hacc": ("psum", [P, 512], "float32"),
    "lE": ("sbuf", [P, W], "float32"),
    "mO": ("sbuf", [P, W], "float32"),
    "junk": ("sbuf", [P, W], "float32"),
    "qown": ("sbuf", [P, 4], "float32"),
    "qland": ("sbuf", [P, 8], "float32"),
    "ones": ("sbuf", [P, P], "float32"),
    "c16": ("sbuf", [P, 32], "float32"),
    "thr2": ("sbuf", [P, 64], "float32"),
    "clampv": ("sbuf", [P, 8], "float32"),
    "asrc": ("sbuf", [P, 32], "float32"),
    "mrow": ("sbuf", [P, 96], "float32"),
    "drow": ("sbuf", [P, 96], "float32"),
    "orow": ("sbuf", [P, 96], "float32"),
    "coef": ("sbuf", [P, 32], "float32"),
    "hrow": ("sbuf", [P, 32], "float32"),
    "yo": ("sbuf", [P, F], "float32"),
    "accA": ("psum", [P, 512], "float32"),
    "accB": ("psum", [P, 512], "float32"),
    "ps": ("psum", [P, 512], "float32"),
}
SEMAPHORES = ["ldA", "ldB", "snd", "tab", "tabr", "a0", "a1", "a23", "late_o", "late_m", "qarr", "vs", "vb", "w0", "cv",
              "cst", "acts", "mms", "st"]


def _bits(mask):
    return [1 << b for b in range(mask.bit_length()) if (mask >> b) & 1]


def _cnt(mask):
    return len(_bits(mask))


def _plan(T, topo):
    cores = list(T.cores)
    info = {}
    for r, c in enumerate(cores):
        mate = [d for d in cores if topo.mates(topo.chip(c), topo.chip(d))][0]
        helper = [h for h in range(min(cores) - P, max(cores) + P)
                  if h >= 0 and h not in cores and topo.chip(h) == topo.chip(c) and topo.die(h) == topo.die(c)
                  and topo.may_write(h, mate)][0]
        lo = min(r, cores.index(mate))
        info[c] = {"rank": r, "mate": mate, "helper": helper, "off": F * lo, "half": r - lo}
    for c in cores:
        mem = [d for d in cores if d == c or topo.same_plane(topo.chip(c), topo.chip(d))]
        mem.sort(key=lambda d: info[d]["off"])
        info[c]["members"] = mem
    return info


def _dst(topo, c):
    rid, pid, _ = topo.addr(c)
    return DstId(rid=rid, pnc=pid)


def _chain(queue, sem):
    n = [0]

    def run(make):
        if n[0]:
            queue.wait_ge(sem, n[0])
        make().then_inc(sem, 1)
        n[0] += 1
        return n[0]
    return run


def _helper_program(g, core, T, topo, own, mate):
    v = g.vector
    S = T.sem
    vop = _chain(v, S.vs)
    low = topo.mask(core, mate)
    high = topo.mask(core, own) & ~low
    add = AluOpType.add
    acc = T.hacc[:, 0:W]

    n = vop(lambda: v.memset(T.ones[:], 1.0))
    g.wait_ge(S.vs, n)
    g.remote_dma_fused([
        RemoteDMATransfer(dst_ids=[_dst(topo, own)], dma_engine_mask=low | high, remote_sem=S.tab,
                          src=T.ones[:], dst=T.ones[:]),
    ], local_sem=S.snd)

    v.wait_ge(S.a23, _cnt(low))
    vop(lambda: v.tensor_tensor(acc, T.hx2[:], T.hx3[:], add))
    v.wait_ge(S.a0, _cnt(high))
    vop(lambda: v.tensor_tensor(acc, acc, T.hp0[:], add))
    v.wait_ge(S.a1, _cnt(low))
    n = vop(lambda: v.tensor_tensor(T.hE[:], acc, T.hx1[:], add))
    g.wait_ge(S.vs, n)
    g.remote_dma_fused([
        RemoteDMATransfer(dst_ids=[_dst(topo, mate)], dma_engine_mask=low, remote_sem=S.late_m, src=T.hE[:], dst=T.mO[:]),
        RemoteDMATransfer(dst_ids=[_dst(topo, own)], dma_engine_mask=high, remote_sem=S.late_o, src=T.hE[:], dst=T.lE[:]),
    ], local_sem=S.snd)
    g.wait_ge(S.snd, 2 * (_cnt(low) + _cnt(high)))


def _rank_program(g, core, T, topo, info):
    me = info[core]
    mem = me["members"]
    i = mem.index(core)
    peer = [mem[i ^ j] for j in range(4)]
    off = [info[c]["off"] for c in peer]
    helper = [info[c]["helper"] for c in peer]
    v, sc, te, sy = g.vector, g.scalar, g.tensor, g.sync
    S = T.sem
    A = AluOpType
    Act = ActivationFunctionType
    vop = _chain(v, S.vs)
    low = topo.mask(core, helper[1])
    high = topo.mask(core, helper[0]) & ~low
    lb = _bits(low)
    low_a, low_b = sum(lb[:len(lb) // 2]), sum(lb[len(lb) // 2:])
    bound = float(T.tables["BOUND"])

    oa, ob = min(off[2], off[3]), min(off[0], off[1])
    sy.dma_start(T.gin[:, oa:oa + 2 * W], T.gr[:, oa:oa + 2 * W]).then_inc(S.ldA, 16)
    sc.dma_start(T.gin[:, ob:ob + 2 * W], T.gr[:, ob:ob + 2 * W]).then_inc(S.ldB, 16)

    v.memset(T.asrc[:], 1.0).then_inc(S.w0, 1)
    g.wait_ge(S.w0, 1)
    g.remote_dma_fused([
        RemoteDMATransfer(dst_ids=[_dst(topo, peer[1])], dma_engine_mask=low, remote_sem=S.tabr,
                          src=T.asrc[:], dst=T.mrow[:, TC + 2:TC + 2 + 32]),
    ], local_sem=S.snd)

    g.wait_ge(S.ldA, 16)
    g.remote_dma_fused([
        RemoteDMATransfer(dst_ids=[_dst(topo, helper[2])], dma_engine_mask=low_a, remote_sem=S.a23,
                          src=T.gin[:, off[2]:off[2] + W], dst=T.hx2[:]),
        RemoteDMATransfer(dst_ids=[_dst(topo, helper[3])], dma_engine_mask=low_b, remote_sem=S.a23,
                          src=T.gin[:, off[3]:off[3] + W], dst=T.hx3[:]),
    ], local_sem=S.snd)
    g.wait_ge(S.ldB, 16)
    g.remote_dma_fused([
        RemoteDMATransfer(dst_ids=[_dst(topo, helper[1])], dma_engine_mask=low, remote_sem=S.a1,
                          src=T.gin[:, off[1]:off[1] + W], dst=T.hx1[:]),
        RemoteDMATransfer(dst_ids=[_dst(topo, helper[0])], dma_engine_mask=high, remote_sem=S.a0,
                          src=T.gin[:, off[0]:off[0] + W], dst=T.hp0[:]),
    ], local_sem=S.snd)

    fills = [(T.c16[:], 16.0), (T.drow[:, 0:TC + 1], 0.0), (T.clampv[:, 0:7], 0.0), (T.clampv[:, 7:8], 1.0),
             (T.mrow[:, TC + 1:TC + 2], 1.0 / 7.5)]
    fills += [(T.coef[:, k:k + 1], COEF[k]) for k in range(NC)]
    for ap, val in fills:
        v.memset(ap, val).then_inc(S.cv, 1)
    v.wait_ge(S.cv, len(fills))
    for k in range(2):
        v.tensor_tensor_scan(T.thr2[:, k * K:(k + 1) * K], T.c16[:, 0:K], T.drow[:, 0:K], 1.0, A.mult, A.add).then_inc(S.cv, 1)
    sc.wait_ge(S.w0, 1)
    for k in range(NC):
        sc.activation(T.drow[:, TC + 1 + k:TC + 2 + k], T.asrc[:, 0:1], Act.Identity, bias=SHIFT[k],
                      scale=0.0).then_inc(S.cst, 1)

    accs = (T.accA[:, 0:F], T.accB[:, 0:F])
    sc.wait_ge(S.late_o, _cnt(high))
    sc.activation(accs[0], T.lE[:, 0:F], Act.Copy).then_inc(S.acts, 1)
    sc.activation(accs[1], T.lE[:, F:W], Act.Copy).then_inc(S.acts, 1)
    v.wait_ge(S.cv, len(fills) + 2)
    v.wait_ge(S.cst, NC)
    v.wait_ge(S.tabr, _cnt(low))
    v.wait_ge(S.late_m, _cnt(low))
    v.wait_ge(S.acts, 1)
    n = vop(lambda: v.tensor_tensor(accs[0], accs[0], T.mO[:, 0:F], A.add))
    v.wait_ge(S.acts, 2)
    v.tensor_tensor(accs[1], accs[1], T.mO[:, F:W], A.add).then_inc(S.vb, 1)
    sc.wait_ge(S.vs, n)
    sc.activation(T.junk[:, 0:F], accs[0], Act.Square, scale=1.0 / bound, accum_out=T.qown[:, 0:1]).then_inc(S.acts, 1)
    sc.wait_ge(S.vb, 1)
    sc.activation(T.junk[:, F:W], accs[1], Act.Square, scale=1.0 / bound, accum_out=T.qown[:, 1:2]).then_inc(S.acts, 1)

    g.wait_ge(S.acts, 4)
    g.remote_dma_fused([
        RemoteDMATransfer(dst_ids=[_dst(topo, peer[j]) for j in (1, 2, 3)], dma_engine_mask=low, remote_sem=S.qarr,
                          srcs=[T.qown[:, 0:2]], dsts=[T.qland[:, 2 * j - 2:2 * j] for j in (1, 2, 3)]),
    ], local_sem=S.snd)

    te.wait_ge(S.tab, _cnt(low) + _cnt(high))
    te.wait_ge(S.acts, 4)
    te.matmul(T.ps[:, 0:2], T.ones[:], T.qown[:, 0:2], True, True).then_inc(S.mms, 1)
    te.wait_ge(S.qarr, 3 * _cnt(low))
    te.matmul(T.ps[:, 2:8], T.ones[:], T.qland[:, 0:6], True, True).then_inc(S.mms, 1)

    t, y0, hv = T.mrow[:, TC:TC + 1], T.orow[:, K - 1:K], T.hrow[:, NC - 1:NC]
    v.wait_ge(S.mms, 2)
    vop(lambda: v.tensor_tensor_scan(T.mrow[:, TC - 7:TC + 1], T.ps[:, 0:8], T.clampv[:], 0.0, A.add, A.max))
    vop(lambda: v.tensor_scalar(T.mrow[:, 0:TC], T.thr2[:, 0:TC], t, 0.25, A.is_gt, A.max))
    vop(lambda: v.tensor_tensor_scan(T.orow[:, 0:L], T.mrow[:, 0:L], T.drow[:, 0:L], 1.0, A.mult, A.add))
    vop(lambda: v.tensor_tensor_scan(T.hrow[:, 0:NC], T.orow[:, TC + 1:L], T.coef[:, 0:NC], 0.0, A.mult, A.add))
    n_out = vop(lambda: v.tensor_scalar(T.yo[:], accs[me["half"]], y0, hv, A.mult, A.mult))

    sy.wait_ge(S.vs, n_out)
    sy.dma_start(T.y[:], T.yo[:]).then_inc(S.st, 16)
    sy.wait_ge(S.st, 16)
    g.wait_ge(S.snd, _cnt(low) + _cnt(low_a) + _cnt(low_b) + _cnt(low) + _cnt(high) + _cnt(low))


def rank_program(g, core, T, topo):
    info = _plan(T, topo)
    if core in info:
        _rank_program(g, core, T, topo, info)
        return
    for c in info:
        if info[c]["helper"] == core:
            _helper_program(g, core, T, topo, c, info[c]["mate"])
            return
